import numpy as np, ml_dtypes
CORES = [48,51,52,55]
N = 4
import mx_ref
BF = ml_dtypes.bfloat16
def entries(a):
    return np.ascontiguousarray(a.T).reshape(-1)
def table(e):
    return np.ascontiguousarray(np.reshape(e, (-1, 16)).T).astype(np.int32)
def cols(t, e):
    v = np.concatenate([t.reshape(128, -1, 4), np.zeros((128, 1, 4), BF)], axis=1)
    return np.ascontiguousarray(v[:, e]).reshape(128, -1)
def pick(q, e):
    c = np.concatenate([q[0].reshape(128, -1, 4), np.zeros((128, 1, 4), np.uint8)], axis=1); s = np.concatenate([q[1], np.ones((16, 1), np.uint8)], axis=1)
    return (np.ascontiguousarray(c[:, e].reshape(128, -1)), np.ascontiguousarray(s[:, e]))
def join(*qs):
    return (np.concatenate([q[0] for q in qs], axis=1), np.concatenate([q[1] for q in qs], axis=1))
def put(q, e, v):
    c, s = q[0].reshape(128, -1, 4).copy(), q[1].copy(); c[:, e] = v[0].reshape(128, -1, 4); s[:, e] = v[1]
    return (c.reshape(128, -1), s)
def pk(c, s):
    return (np.ascontiguousarray(c), mx_ref.live(s))
def emit(q):
    return q[0], q[1]
def decode(q):
    o = []
    for b in range(4):
        e = np.zeros((128, 128, 4), np.float32); e[np.arange(128), np.arange(128), b] = 1
        o.append(mx_ref.matmul(mx_ref.quantize(e.reshape(128, 512).astype(BF)), q))
    return np.stack(o, axis=2).reshape(128, -1)
def f(rng, *shape):
    return mx_ref.flush((rng.standard_normal(shape, dtype=np.float32) * np.exp2(rng.integers(-2, 3, shape[:-1] + (1,)))).astype(BF))
def wide(rng, *shape, cols=0):
    v = rng.standard_normal(shape, dtype=np.float32) * np.exp2(rng.integers(-12, 13, shape)).astype(np.float32)
    if cols: v *= np.repeat(np.exp2(rng.integers(-cols, cols + 1, shape[:-2] + (1, shape[-1] // 4))) * (rng.random(shape[:-2] + (1, shape[-1] // 4)) > 0.0625), 4, axis=-1).astype(np.float32)
    return mx_ref.flush(v.astype(BF))
T, CAPP = 512, 128
def lists(rng, count, high=False, among=T, unnamed=0):
    sn, so = np.full((N, N * CAPP), -1), np.zeros((N, 512), int)
    for d in range(N):
        filled = []
        for s in range(N):
            c = np.sort(rng.permutation(CAPP)[:count[s, d]]); k = rng.permutation(among)[:c.size]
            sn[s, d * CAPP + c] = np.sort(k)[::-1] if high else k
            filled.append(s * CAPP + c)
        filled = np.concatenate(filled)
        if unnamed: filled = rng.permutation(filled)[unnamed:]
        o = np.concatenate([filled, rng.choice(filled, 512 - filled.size)])
        so[d] = np.sort(o)[::-1] if high else rng.permutation(o)
    return {"sn": np.stack([table(v) for v in sn]), "so": np.stack([table(v) for v in so])}
def setup_inputs(rng):
    return {"x": f(rng, N, 128, 4 * T), **lists(rng, rng.integers(1, CAPP + 1, (N, N)))}
def setup_inputs_full(rng):
    return {**setup_inputs(rng), **lists(rng, np.full((N, N), CAPP))}
def setup_inputs_one(rng):
    n = np.zeros((N, N), int); n[rng.integers(0, N)] = 3
    return {**setup_inputs(rng), **lists(rng, n, among=rng.permutation(T)[:3])}
def setup_inputs_own(rng):
    return {**setup_inputs(rng), **lists(rng, CAPP * np.eye(N, dtype=int))}
def setup_inputs_reversed(rng):
    return {**setup_inputs(rng), **lists(rng, rng.integers(1, CAPP + 1, (N, N)), high=True, unnamed=3)}
def setup_inputs_spread(rng):
    d = setup_inputs(rng); d["x"] = wide(rng, N, 128, 4 * T, cols=8); return d
def check_inputs(d):
    b = []
    a = np.stack([entries(d["sn"][s]) for s in range(N)])
    for r in range(N):
        pairs = [a[r, q * CAPP:q * CAPP + CAPP] for q in range(N)]
        if a[r].min() < -1 or a[r].max() >= T or any(len(set(g[g >= 0].tolist())) != (g >= 0).sum() for g in pairs): b.append("sn")
        e = entries(d["so"][r])
        if e.min() < 0 or e.max() >= N * CAPP: b.append("so")
        elif (a[e // CAPP, r * CAPP + e % CAPP] < 0).any(): b.append("so")
    return b
def reference(x, sn, so):
    v = np.concatenate([x[s] for s in range(N)], axis=1)
    a = np.stack([entries(sn[s]) for s in range(N)])
    fc, fs = np.zeros((N, 128, 2048), np.uint8), np.zeros((N, 16, 512), np.uint8)
    bc, bs = np.zeros((N, 128, 2048), np.uint8), np.zeros((N, 16, 512), np.uint8)
    for d in range(N):
        e = entries(so[d]); s = e // CAPP
        F = mx_ref.quantize(cols(v, s * T + a[s, d * CAPP + e % CAPP]))
        fc[d], fs[d] = emit(F)
        m = decode(F).reshape(128, 512, 4).transpose(0, 2, 1).reshape(512, 512)
        m = np.ascontiguousarray(m.T).astype(BF)
        bt = []
        for b in range(4):
            k = np.ascontiguousarray(m[:, 128 * b:128 * b + 128]).reshape(128, 4, 128)
            bt.append(mx_ref.quantize(np.ascontiguousarray(k.transpose(0, 2, 1)).reshape(128, 512)))
        bc[d], bs[d] = emit(join(*bt))
    return {"fc": fc, "fs": fs, "bc": bc, "bs": bs}

@@ -1,0 +1,232 @@
+from concourse.bass import DstId, RemoteDMATransfer
+from concourse.mybir import dt, AluOpType, ActivationFunctionType
+
+N = 4
+CAPP = 128
+TOK = 512
+XA = 384
+RUNS = ((0, 320), (320, 512))
+COPY_V = ((0, 2), (0, 3), (1, 0), (1, 3))
+COPY_S = ((0, 0), (0, 1), (1, 1), (1, 2))
+
+SCRATCH = {
+    "xt": ("sbuf", [128, 4 * TOK], "bfloat16"),
+    "sn8": ("sbuf", [128, 32], "int32"),
+    "lst": ("sbuf", [128, 32], "uint16"),
+    "dm": ("dram", [4, 520], "int32"),
+    "m2": ("sbuf", [128, 128], "int32"),
+    "lp": ("sbuf", [128, 32], "uint16"),
+    "zi": ("sbuf", [128, 32], "int32"),
+    "ca": ("sbuf", [128, 32], "int32"),
+    "cb": ("sbuf", [128, 32], "int32"),
+    "cc": ("sbuf", [128, 32], "int32"),
+    "cl": ("sbuf", [128, 32], "uint16"),
+    "ones": ("sbuf", [128, 128], "bfloat16"),
+    "ident": ("sbuf", [128, 128], "bfloat16"),
+    "et": ("sbuf", [128, 2048], "bfloat16"),
+    "pp": ("psum", [128, 4096], "float32"),
+    "bt": ("sbuf", [128, 2048], "bfloat16"),
+}
+for _n, _w in (("x", 512), ("slot", 384), ("land", 512), ("e", 512), ("fp", 512), ("fn", 512), ("bt", 512)):
+    SCRATCH[_n + "q"] = ("sbuf", [128, _w], "float8_e4m3fn_x4")
+    SCRATCH[_n + "s"] = ("sbuf", [128, _w], "uint8")
+SEMAPHORES = (
+    ["x0", "x1", "snl", "dml", "m2l", "stsy", "stsc",
+     "vones", "vez", "gid", "gz", "vec", "veq", "qx", "vlst", "pkc", "pks", "ownc", "owns",
+     "vca", "vcc", "vcl", "vlp", "snd", "arrc", "arrs", "vn", "sn2", "q0", "q1", "cv0", "cv1", "cs0", "cs1"]
+    + ["fc%d" % t for t in range(4)] + ["fs%d" % t for t in range(4)]
+    + ["mm%d%d" % (h, t) for h in range(2) for t in range(4)])
+
+
+def send_masks(src, cores, topo):
+    far = [c for c in cores if c != src and topo.die(c) != topo.die(src)]
+    near = [c for c in cores if c != src and topo.die(c) == topo.die(src)]
+    plan = {}
+    for group, first in ((far, 0), (near, 1)):
+        for i, c in enumerate(group):
+            e = topo.engines(src, c)
+            half = (e[first::2], e[1 - first::2])
+            k = len(half[0]) // len(group)
+            plan[c] = (half[0][i * k:(i + 1) * k], half[1][i * k:(i + 1) * k])
+    return plan
+
+
+def bits(engines):
+    m = 0
+    for e in engines:
+        m |= 1 << e
+    return m
+
+
+def rank_program(g, core, T, topo):
+    rank = T.rank_of(core)
+    if rank is None:
+        return
+    S = T.sem
+    v, sc, te, sy = g.vector, g.scalar, g.tensor, g.sync
+    Copy = ActivationFunctionType.Copy
+    u32, u8 = dt.uint32, dt.uint8
+    order = [(rank + 1 + i) % N for i in range(N)]
+
+    sy.dma_start(T.xt[:, 0:4 * XA], T.x[:, 0:4 * XA]).then_inc(S.x0, 16)
+    sy.dma_start(T.xt[:, 4 * XA:4 * TOK], T.x[:, 4 * XA:4 * TOK]).then_inc(S.x1, 16)
+    for k in range(8):
+        sc.dma_start(T.sn8[16 * k:16 * k + 16, :], T.sn[:]).then_inc(S.snl, 16)
+    for q in range(4):
+        sy.dma_start(T.dm[q:q + 1, 4 - q:516 - q], T.so[:]).then_inc(S.dml, 16)
+    for q in range(1, 4):
+        sy.dma_start(T.dm[q:q + 1, 516 - q:518], T.so[0:1, 0:2 + q]).then_inc(S.dml, 16)
+    sy.wait_ge(S.dml, 112)
+    for k in range(8):
+        sy.dma_start(T.m2[16 * k:16 * k + 16, :], T.dm[0:4, 4:516]).then_inc(S.m2l, 16)
+
+    v.memset(T.ones[:], 1.0).then_inc(S.vones, 1)
+    v.memset(T.et[:], 0.0).then_inc(S.vez, 1)
+    g.wait_ge(S.vones, 1)
+    g.affine_select(T.ident[:], T.ones[:], [[-1, 128]], AluOpType.is_equal, 0.0, 0, 1).then_inc(S.gid, 1)
+    g.iota(T.zi[:], [[4, 32]], 0, 128).then_inc(S.gz, 1)
+    v.wait_ge(S.vez, 1)
+    v.wait_ge(S.gid, 1)
+    for t in range(4):
+        v.tensor_copy(T.et[:, 5 * t:2048:16], T.ident[:]).then_inc(S.vec, 1)
+
+    v.wait_ge(S.x0, 16)
+    v.quantize_mx(T.xq[:, 0:XA], T.xs[:, 0:XA], T.xt[:, 0:4 * XA]).then_inc(S.qx, 1)
+    v.wait_ge(S.snl, 128)
+    a = 8 * (rank + 1)
+    nl = 0
+    if a < 32:
+        v.tensor_copy(T.lst[:, 0:32 - a], T.sn8[:, a:32]).then_inc(S.vlst, 1)
+        nl += 1
+    v.tensor_copy(T.lst[:, 32 - a:32], T.sn8[:, 0:a]).then_inc(S.vlst, 1)
+    nl += 1
+    v.wait_ge(S.x1, 16)
+    v.quantize_mx(T.xq[:, XA:TOK], T.xs[:, XA:TOK], T.xt[:, 4 * XA:4 * TOK]).then_inc(S.qx, 1)
+
+    v.wait_ge(S.vlst, nl)
+    v.wait_ge(S.qx, 2)
+    v.tensor_copy(T.slotq[:, 0:384].bitcast(u32),
+                  T.xq[:, 0:TOK].bitcast(u32).indirect(T.lst[:, 0:24])).then_inc(S.pkc, 1)
+    own = CAPP * rank
+    v.tensor_copy(T.landq[:, own:own + CAPP].bitcast(u32),
+                  T.xq[:, 0:TOK].bitcast(u32).indirect(T.lst[:, 24:32])).then_inc(S.ownc, 1)
+    sc.wait_ge(S.vlst, nl)
+    sc.wait_ge(S.qx, 2)
+    sc.activation(T.slots[:, 0:384], T.xs[:, 0:TOK].indirect(T.lst[:, 0:24]), Copy).then_inc(S.pks, 1)
+    sc.activation(T.lands[:, own:own + CAPP], T.xs[:, 0:TOK].indirect(T.lst[:, 24:32]), Copy).then_inc(S.owns, 1)
+
+    plan = send_masks(core, T.cores, topo)
+    tc, ts, sent = [], [], 0
+    for i, d in enumerate(order[:3]):
+        dst = T.cores[d]
+        rid, pid, _ = topo.addr(dst)
+        to = [DstId(rid=rid, pnc=pid)]
+        ec, es = plan[dst]
+        tc.append(RemoteDMATransfer(dst_ids=to, dma_engine_mask=bits(ec), remote_sem=S.arrc,
+                                    src=T.slotq[:, CAPP * i:CAPP * (i + 1)].bitcast(u8),
+                                    dst=T.landq[:, own:own + CAPP].bitcast(u8)))
+        ts.append(RemoteDMATransfer(dst_ids=to, dma_engine_mask=bits(es), remote_sem=S.arrs,
+                                    src=T.slots[:, CAPP * i:CAPP * (i + 1)],
+                                    dst=T.lands[:, own:own + CAPP]))
+        sent += len(ec) + len(es)
+    g.wait_ge(S.pkc, 1)
+    g.remote_dma_fused(tc, local_sem=S.snd)
+    g.wait_ge(S.pks, 1)
+    g.remote_dma_fused(ts, local_sem=S.snd)
+    g.wait_ge(S.snd, sent)
+    inc, ins = 0, 0
+    for d in order[:3]:
+        ec, es = send_masks(T.cores[d], T.cores, topo)[core]
+        inc += len(ec)
+        ins += len(es)
+
+    v.wait_ge(S.vec, 4)
+    v.quantize_mx(T.eq[:, 0:512], T.es[:, 0:512], T.et[:, 0:2048]).then_inc(S.veq, 1)
+    v.wait_ge(S.gz, 1)
+    v.tensor_scalar(T.ca[:], T.zi[:], 508, None, AluOpType.bitwise_and).then_inc(S.vca, 1)
+    v.tensor_scalar(T.cb[:], T.zi[:], 9, 3, AluOpType.logical_shift_right, AluOpType.bitwise_and).then_inc(S.vca, 1)
+    v.wait_ge(S.vca, 2)
+    v.tensor_tensor(T.cc[:], T.ca[:], T.cb[:], AluOpType.add).then_inc(S.vcc, 1)
+    v.wait_ge(S.vcc, 1)
+    v.tensor_copy(T.cl[:], T.cc[:]).then_inc(S.vcl, 1)
+    v.wait_ge(S.m2l, 128)
+    v.tensor_copy(T.lp[:], T.m2[:, 0:128:4]).then_inc(S.vlp, 1)
+
+    te.wait_ge(S.veq, 1)
+    for h, (lo, hi) in enumerate(RUNS):
+        for t in range(4):
+            if h == 0:
+                te.wait_ge(S["fc%d" % t], 1)
+                te.wait_ge(S["fs%d" % t], 1)
+            b = 512 * (4 * h + t)
+            te.matmul_mx(T.pp[:, b:b + hi - lo], T.fpq[:, 128 * t:128 * t + 128], T.fps[:, 128 * t:128 * t + 128],
+                         T.eq[:, lo:hi], T.es[:, lo:hi], True, True).then_inc(S["mm%d%d" % (h, t)], 1)
+
+    def copy_v(h, t):
+        lo, hi = RUNS[h]
+        b = 512 * (4 * h + t)
+        v.wait_ge(S["mm%d%d" % (h, t)], 1)
+        v.tensor_copy(T.bt[:, 4 * lo + t:4 * hi:4], T.pp[:, b:b + hi - lo]).then_inc(S["cv%d" % h], 1)
+
+    def copy_s(h, t):
+        lo, hi = RUNS[h]
+        b = 512 * (4 * h + t)
+        sc.wait_ge(S["mm%d%d" % (h, t)], 1)
+        sc.activation(T.bt[:, 4 * lo + t:4 * hi:4], T.pp[:, b:b + hi - lo], Copy).then_inc(S["cs%d" % h], 1)
+
+    v.wait_ge(S.vlp, 1)
+    v.wait_ge(S.ownc, 1)
+    v.wait_ge(S.arrc, inc)
+    for t in range(4):
+        v.tensor_copy(T.fpq[:, 128 * t:128 * t + 128].bitcast(u32),
+                      T.landq[:, 0:512].bitcast(u32).indirect(T.lp[:, 8 * t:8 * t + 8])).then_inc(S["fc%d" % t], 1)
+    v.wait_ge(S.vcl, 1)
+    for t in range(4):
+        v.wait_ge(S["fc%d" % t], 1)
+    v.tensor_copy(T.fnq[:, 0:512].bitcast(u32),
+                  T.fpq[:, 0:512].bitcast(u32).indirect(T.cl[:, 0:32])).then_inc(S.vn, 1)
+    for h, (lo, hi) in enumerate(RUNS):
+        for hh, t in COPY_V:
+            if hh == h:
+                copy_v(h, t)
+        v.wait_ge(S["cv%d" % h], sum(1 for c in COPY_V if c[0] == h))
+        v.wait_ge(S["cs%d" % h], sum(1 for c in COPY_S if c[0] == h))
+        v.quantize_mx(T.btq[:, lo:hi], T.bts[:, lo:hi], T.bt[:, 4 * lo:4 * hi]).then_inc(S["q%d" % h], 1)
+
+    sc.wait_ge(S.vlp, 1)
+    sc.wait_ge(S.owns, 1)
+    sc.wait_ge(S.arrs, ins)
+    for t in range(4):
+        sc.activation(T.fps[:, 128 * t:128 * t + 128],
+                      T.lands[:, 0:512].indirect(T.lp[:, 8 * t:8 * t + 8]), Copy).then_inc(S["fs%d" % t], 1)
+    for h, t in COPY_S:
+        if h == 0:
+            copy_s(h, t)
+    sc.wait_ge(S.vcl, 1)
+    for t in range(4):
+        sc.wait_ge(S["fs%d" % t], 1)
+    sc.activation(T.fns[:, 0:512], T.fps[:, 0:512].indirect(T.cl[:, 0:32]), Copy).then_inc(S.sn2, 1)
+    for h, t in COPY_S:
+        if h == 1:
+            copy_s(h, t)
+
+    def store_bc(h):
+        lo, hi = RUNS[h]
+        sy.wait_ge(S["q%d" % h], 1)
+        sy.dma_start(T.bc[:, 4 * lo:4 * hi], T.btq[:, lo:hi].bitcast(u8)).then_inc(S.stsy, 16)
+
+    sy.wait_ge(S.vn, 1)
+    sy.dma_start(T.fc[:, 0:2048], T.fnq[:, 0:512].bitcast(u8)).then_inc(S.stsy, 16)
+    store_bc(0)
+    sy.wait_ge(S.sn2, 1)
+    for k in range(4):
+        sy.dma_start(T.fs[4 * k:4 * k + 4, 0:512], T.fns[32 * k:32 * k + 4, 0:512]).then_inc(S.stsy, 16)
+    store_bc(1)
+    sy.wait_ge(S.q0, 1)
+    sy.dma_start(T.bs[12:16, 0:512], T.bts[96:100, 0:512]).then_inc(S.stsy, 16)
+    sc.wait_ge(S.q0, 1)
+    sc.wait_ge(S.q1, 1)
+    for k in range(3):
+        sc.dma_start(T.bs[4 * k:4 * k + 4, 0:512], T.bts[32 * k:32 * k + 4, 0:512]).then_inc(S.stsc, 16)
+    sy.wait_ge(S.stsy, 16 * 8)
+    sc.wait_ge(S.stsc, 16 * 3)

@@ -4,17 +4,17 @@ from concourse.mybir import dt, AluOpType, ActivationFunctionType
 N = 4
 CAPP = 128
 TOK = 512
-XA = 384
+XA = 336
 RUNS = ((0, 320), (320, 512))
 COPY_V = ((0, 2), (0, 3), (1, 0), (1, 3))
 COPY_S = ((0, 0), (0, 1), (1, 1), (1, 2))
 
 SCRATCH = {
     "xt": ("sbuf", [128, 4 * TOK], "bfloat16"),
-    "sn8": ("sbuf", [128, 32], "int32"),
+    "sn2": ("sbuf", [32, 32], "int32"),
     "lst": ("sbuf", [128, 32], "uint16"),
     "dm": ("dram", [4, 520], "int32"),
-    "m2": ("sbuf", [128, 128], "int32"),
+    "m2": ("sbuf", [32, 128], "int32"),
     "lp": ("sbuf", [128, 32], "uint16"),
     "zi": ("sbuf", [128, 32], "int32"),
     "ca": ("sbuf", [128, 32], "int32"),
@@ -27,28 +27,31 @@ SCRATCH = {
     "pp": ("psum", [128, 4096], "float32"),
     "bt": ("sbuf", [128, 2048], "bfloat16"),
 }
-for _n, _w in (("x", 512), ("slot", 384), ("land", 512), ("e", 512), ("fp", 512), ("fn", 512), ("bt", 512)):
+for _n, _w in (("x", 512), ("slot", 512), ("land", 512), ("e", 512), ("fp", 512), ("fn", 512), ("bt", 512)):
     SCRATCH[_n + "q"] = ("sbuf", [128, _w], "float8_e4m3fn_x4")
     SCRATCH[_n + "s"] = ("sbuf", [128, _w], "uint8")
 SEMAPHORES = (
     ["x0", "x1", "snl", "dml", "m2l", "stsy", "stsc",
-     "vones", "vez", "gid", "gz", "vec", "veq", "qx", "vlst", "pkc", "pks", "ownc", "owns",
-     "vca", "vcc", "vcl", "vlp", "snd", "arrc", "arrs", "vn", "sn2", "q0", "q1", "cv0", "cv1", "cs0", "cs1"]
+     "vones", "vez", "sez", "gid", "gz", "sec", "veq", "qx", "vlst", "ownc", "owns",
+     "vca", "vcc", "vcl", "vlp", "snd", "arrc", "arrs", "fnc", "fnsc", "q0", "q1", "cv0", "cv1", "cs0", "cs1"]
+    + ["pc%d" % i for i in range(3)] + ["ps%d" % i for i in range(3)]
     + ["fc%d" % t for t in range(4)] + ["fs%d" % t for t in range(4)]
     + ["mm%d%d" % (h, t) for h in range(2) for t in range(4)])
 
 
-def send_masks(src, cores, topo):
-    far = [c for c in cores if c != src and topo.die(c) != topo.die(src)]
-    near = [c for c in cores if c != src and topo.die(c) == topo.die(src)]
-    plan = {}
-    for group, first in ((far, 0), (near, 1)):
-        for i, c in enumerate(group):
-            e = topo.engines(src, c)
-            half = (e[first::2], e[1 - first::2])
-            k = len(half[0]) // len(group)
-            plan[c] = (half[0][i * k:(i + 1) * k], half[1][i * k:(i + 1) * k])
-    return plan
+def receivers(src, cores, topo):
+    mine = [c for c in cores if topo.die(c) == topo.die(src)]
+    far = [c for c in cores if topo.die(c) != topo.die(src)]
+    k = mine.index(src)
+    far = far[k:] + far[:k]
+    near = [c for c in mine if c != src]
+    out = []
+    for i, c in enumerate(far[:1] + near + far[1:]):
+        e = topo.engines(src, c)
+        a, b = e[0::2], e[1::2]
+        h = len(b) // 2
+        out.append((c, (a, b, a)[i], (b[:h], a, b[h:])[i]))
+    return out
 
 
 def bits(engines):
@@ -66,82 +69,31 @@ def rank_program(g, core, T, topo):
     v, sc, te, sy = g.vector, g.scalar, g.tensor, g.sync
     Copy = ActivationFunctionType.Copy
     u32, u8 = dt.uint32, dt.uint8
-    order = [(rank + 1 + i) % N for i in range(N)]
 
+    for k, q in enumerate((sy, sc)):
+        q.dma_start(T.sn2[16 * k:16 * k + 16, :], T.sn[:]).then_inc(S.snl, 16)
     sy.dma_start(T.xt[:, 0:4 * XA], T.x[:, 0:4 * XA]).then_inc(S.x0, 16)
     sy.dma_start(T.xt[:, 4 * XA:4 * TOK], T.x[:, 4 * XA:4 * TOK]).then_inc(S.x1, 16)
-    for k in range(8):
-        sc.dma_start(T.sn8[16 * k:16 * k + 16, :], T.sn[:]).then_inc(S.snl, 16)
     for q in range(4):
-        sy.dma_start(T.dm[q:q + 1, 4 - q:516 - q], T.so[:]).then_inc(S.dml, 16)
+        sc.dma_start(T.dm[q:q + 1, 4 - q:516 - q], T.so[:]).then_inc(S.dml, 16)
     for q in range(1, 4):
-        sy.dma_start(T.dm[q:q + 1, 516 - q:518], T.so[0:1, 0:2 + q]).then_inc(S.dml, 16)
+        sc.dma_start(T.dm[q:q + 1, 516 - q:518], T.so[0:1, 0:2 + q]).then_inc(S.dml, 16)
     sy.wait_ge(S.dml, 112)
-    for k in range(8):
+    for k in range(2):
         sy.dma_start(T.m2[16 * k:16 * k + 16, :], T.dm[0:4, 4:516]).then_inc(S.m2l, 16)
 
     v.memset(T.ones[:], 1.0).then_inc(S.vones, 1)
-    v.memset(T.et[:], 0.0).then_inc(S.vez, 1)
+    v.memset(T.et[:, 0:1024], 0.0).then_inc(S.vez, 1)
     g.wait_ge(S.vones, 1)
-    g.affine_select(T.ident[:], T.ones[:], [[-1, 128]], AluOpType.is_equal, 0.0, 0, 1).then_inc(S.gid, 1)
     g.iota(T.zi[:], [[4, 32]], 0, 128).then_inc(S.gz, 1)
-    v.wait_ge(S.vez, 1)
-    v.wait_ge(S.gid, 1)
+    g.affine_select(T.ident[:], T.ones[:], [[-1, 128]], AluOpType.is_equal, 0.0, 0, 1).then_inc(S.gid, 1)
+    sc.wait_ge(S.vez, 1)
+    sc.activation(T.et[:, 1024:2048], T.et[:, 0:1024], Copy).then_inc(S.sez, 1)
+    sc.wait_ge(S.gid, 1)
+    sc.wait_ge(S.sez, 1)
     for t in range(4):
-        v.tensor_copy(T.et[:, 5 * t:2048:16], T.ident[:]).then_inc(S.vec, 1)
+        sc.activation(T.et[:, 5 * t:2048:16], T.ident[:], Copy).then_inc(S.sec, 1)
 
-    v.wait_ge(S.x0, 16)
-    v.quantize_mx(T.xq[:, 0:XA], T.xs[:, 0:XA], T.xt[:, 0:4 * XA]).then_inc(S.qx, 1)
-    v.wait_ge(S.snl, 128)
-    a = 8 * (rank + 1)
-    nl = 0
-    if a < 32:
-        v.tensor_copy(T.lst[:, 0:32 - a], T.sn8[:, a:32]).then_inc(S.vlst, 1)
-        nl += 1
-    v.tensor_copy(T.lst[:, 32 - a:32], T.sn8[:, 0:a]).then_inc(S.vlst, 1)
-    nl += 1
-    v.wait_ge(S.x1, 16)
-    v.quantize_mx(T.xq[:, XA:TOK], T.xs[:, XA:TOK], T.xt[:, 4 * XA:4 * TOK]).then_inc(S.qx, 1)
-
-    v.wait_ge(S.vlst, nl)
-    v.wait_ge(S.qx, 2)
-    v.tensor_copy(T.slotq[:, 0:384].bitcast(u32),
-                  T.xq[:, 0:TOK].bitcast(u32).indirect(T.lst[:, 0:24])).then_inc(S.pkc, 1)
-    own = CAPP * rank
-    v.tensor_copy(T.landq[:, own:own + CAPP].bitcast(u32),
-                  T.xq[:, 0:TOK].bitcast(u32).indirect(T.lst[:, 24:32])).then_inc(S.ownc, 1)
-    sc.wait_ge(S.vlst, nl)
-    sc.wait_ge(S.qx, 2)
-    sc.activation(T.slots[:, 0:384], T.xs[:, 0:TOK].indirect(T.lst[:, 0:24]), Copy).then_inc(S.pks, 1)
-    sc.activation(T.lands[:, own:own + CAPP], T.xs[:, 0:TOK].indirect(T.lst[:, 24:32]), Copy).then_inc(S.owns, 1)
-
-    plan = send_masks(core, T.cores, topo)
-    tc, ts, sent = [], [], 0
-    for i, d in enumerate(order[:3]):
-        dst = T.cores[d]
-        rid, pid, _ = topo.addr(dst)
-        to = [DstId(rid=rid, pnc=pid)]
-        ec, es = plan[dst]
-        tc.append(RemoteDMATransfer(dst_ids=to, dma_engine_mask=bits(ec), remote_sem=S.arrc,
-                                    src=T.slotq[:, CAPP * i:CAPP * (i + 1)].bitcast(u8),
-                                    dst=T.landq[:, own:own + CAPP].bitcast(u8)))
-        ts.append(RemoteDMATransfer(dst_ids=to, dma_engine_mask=bits(es), remote_sem=S.arrs,
-                                    src=T.slots[:, CAPP * i:CAPP * (i + 1)],
-                                    dst=T.lands[:, own:own + CAPP]))
-        sent += len(ec) + len(es)
-    g.wait_ge(S.pkc, 1)
-    g.remote_dma_fused(tc, local_sem=S.snd)
-    g.wait_ge(S.pks, 1)
-    g.remote_dma_fused(ts, local_sem=S.snd)
-    g.wait_ge(S.snd, sent)
-    inc, ins = 0, 0
-    for d in order[:3]:
-        ec, es = send_masks(T.cores[d], T.cores, topo)[core]
-        inc += len(ec)
-        ins += len(es)
-
-    v.wait_ge(S.vec, 4)
-    v.quantize_mx(T.eq[:, 0:512], T.es[:, 0:512], T.et[:, 0:2048]).then_inc(S.veq, 1)
     v.wait_ge(S.gz, 1)
     v.tensor_scalar(T.ca[:], T.zi[:], 508, None, AluOpType.bitwise_and).then_inc(S.vca, 1)
     v.tensor_scalar(T.cb[:], T.zi[:], 9, 3, AluOpType.logical_shift_right, AluOpType.bitwise_and).then_inc(S.vca, 1)
@@ -149,8 +101,53 @@ def rank_program(g, core, T, topo):
     v.tensor_tensor(T.cc[:], T.ca[:], T.cb[:], AluOpType.add).then_inc(S.vcc, 1)
     v.wait_ge(S.vcc, 1)
     v.tensor_copy(T.cl[:], T.cc[:]).then_inc(S.vcl, 1)
-    v.wait_ge(S.m2l, 128)
-    v.tensor_copy(T.lp[:], T.m2[:, 0:128:4]).then_inc(S.vlp, 1)
+    v.wait_ge(S.snl, 32)
+    for k in range(4):
+        v.tensor_copy(T.lst[32 * k:32 * k + 32, :], T.sn2[:]).then_inc(S.vlst, 1)
+    v.wait_ge(S.x0, 16)
+    v.quantize_mx(T.xq[:, 0:XA], T.xs[:, 0:XA], T.xt[:, 0:4 * XA]).then_inc(S.qx, 1)
+    v.wait_ge(S.x1, 16)
+    v.quantize_mx(T.xq[:, XA:TOK], T.xs[:, XA:TOK], T.xt[:, 4 * XA:4 * TOK]).then_inc(S.qx, 1)
+
+    for q in (v, sc):
+        q.wait_ge(S.vlst, 4)
+        q.wait_ge(S.qx, 2)
+
+    def pick(d, code, scale, c_sem, s_sem):
+        lo, hi = CAPP * d, CAPP * (d + 1)
+        off = T.lst[:, 8 * d:8 * d + 8]
+        v.tensor_copy(code[:, lo:hi].bitcast(u32), T.xq[:, 0:TOK].bitcast(u32).indirect(off)).then_inc(c_sem, 1)
+        sc.activation(scale[:, lo:hi], T.xs[:, 0:TOK].indirect(off), Copy).then_inc(s_sem, 1)
+
+    own = slice(CAPP * rank, CAPP * (rank + 1))
+    plan = receivers(core, T.cores, topo)
+    codes, scales = [], []
+    for i, (dst, ec, es) in enumerate(plan):
+        d = T.rank_of(dst)
+        pick(d, T.slotq, T.slots, S["pc%d" % i], S["ps%d" % i])
+        rid, pid, _ = topo.addr(dst)
+        cut = slice(CAPP * d, CAPP * (d + 1))
+        codes.append(RemoteDMATransfer(dst_ids=[DstId(rid=rid, pnc=pid)], dma_engine_mask=bits(ec), remote_sem=S.arrc,
+                                       src=T.slotq[:, cut].bitcast(u8), dst=T.landq[:, own].bitcast(u8)))
+        scales.append(RemoteDMATransfer(dst_ids=[DstId(rid=rid, pnc=pid)], dma_engine_mask=bits(es), remote_sem=S.arrs,
+                                        src=T.slots[:, cut], dst=T.lands[:, own]))
+    pick(rank, T.landq, T.lands, S.ownc, S.owns)
+    g.wait_ge(S.pc0, 1)
+    g.remote_dma_fused(codes[:1], local_sem=S.snd)
+    g.wait_ge(S.pc1, 1)
+    g.wait_ge(S.pc2, 1)
+    g.remote_dma_fused(codes[1:], local_sem=S.snd)
+    for i in range(3):
+        g.wait_ge(S["ps%d" % i], 1)
+    g.remote_dma_fused(scales, local_sem=S.snd)
+    g.wait_ge(S.snd, sum(len(ec) + len(es) for _, ec, es in plan))
+    arrive = [e for src in T.cores for e in receivers(src, T.cores, topo) if e[0] == core]
+
+    v.wait_ge(S.m2l, 32)
+    for k in range(4):
+        v.tensor_copy(T.lp[32 * k:32 * k + 32, :], T.m2[:, 0:128:4]).then_inc(S.vlp, 1)
+    v.wait_ge(S.sec, 4)
+    v.quantize_mx(T.eq[:, 0:512], T.es[:, 0:512], T.et[:, 0:2048]).then_inc(S.veq, 1)
 
     te.wait_ge(S.veq, 1)
     for h, (lo, hi) in enumerate(RUNS):
@@ -174,9 +171,9 @@ def rank_program(g, core, T, topo):
         sc.wait_ge(S["mm%d%d" % (h, t)], 1)
         sc.activation(T.bt[:, 4 * lo + t:4 * hi:4], T.pp[:, b:b + hi - lo], Copy).then_inc(S["cs%d" % h], 1)
 
-    v.wait_ge(S.vlp, 1)
+    v.wait_ge(S.vlp, 4)
     v.wait_ge(S.ownc, 1)
-    v.wait_ge(S.arrc, inc)
+    v.wait_ge(S.arrc, sum(len(ec) for _, ec, _ in arrive))
     for t in range(4):
         v.tensor_copy(T.fpq[:, 128 * t:128 * t + 128].bitcast(u32),
                       T.landq[:, 0:512].bitcast(u32).indirect(T.lp[:, 8 * t:8 * t + 8])).then_inc(S["fc%d" % t], 1)
@@ -184,7 +181,7 @@ def rank_program(g, core, T, topo):
     for t in range(4):
         v.wait_ge(S["fc%d" % t], 1)
     v.tensor_copy(T.fnq[:, 0:512].bitcast(u32),
-                  T.fpq[:, 0:512].bitcast(u32).indirect(T.cl[:, 0:32])).then_inc(S.vn, 1)
+                  T.fpq[:, 0:512].bitcast(u32).indirect(T.cl[:, 0:32])).then_inc(S.fnc, 1)
     for h, (lo, hi) in enumerate(RUNS):
         for hh, t in COPY_V:
             if hh == h:
@@ -193,9 +190,9 @@ def rank_program(g, core, T, topo):
         v.wait_ge(S["cs%d" % h], sum(1 for c in COPY_S if c[0] == h))
         v.quantize_mx(T.btq[:, lo:hi], T.bts[:, lo:hi], T.bt[:, 4 * lo:4 * hi]).then_inc(S["q%d" % h], 1)
 
-    sc.wait_ge(S.vlp, 1)
+    sc.wait_ge(S.vlp, 4)
     sc.wait_ge(S.owns, 1)
-    sc.wait_ge(S.arrs, ins)
+    sc.wait_ge(S.arrs, sum(len(es) for _, _, es in arrive))
     for t in range(4):
         sc.activation(T.fps[:, 128 * t:128 * t + 128],
                       T.lands[:, 0:512].indirect(T.lp[:, 8 * t:8 * t + 8]), Copy).then_inc(S["fs%d" % t], 1)
@@ -205,7 +202,7 @@ def rank_program(g, core, T, topo):
     sc.wait_ge(S.vcl, 1)
     for t in range(4):
         sc.wait_ge(S["fs%d" % t], 1)
-    sc.activation(T.fns[:, 0:512], T.fps[:, 0:512].indirect(T.cl[:, 0:32]), Copy).then_inc(S.sn2, 1)
+    sc.activation(T.fns[:, 0:512], T.fps[:, 0:512].indirect(T.cl[:, 0:32]), Copy).then_inc(S.fnsc, 1)
     for h, t in COPY_S:
         if h == 1:
             copy_s(h, t)
@@ -215,10 +212,10 @@ def rank_program(g, core, T, topo):
         sy.wait_ge(S["q%d" % h], 1)
         sy.dma_start(T.bc[:, 4 * lo:4 * hi], T.btq[:, lo:hi].bitcast(u8)).then_inc(S.stsy, 16)
 
-    sy.wait_ge(S.vn, 1)
+    sy.wait_ge(S.fnc, 1)
     sy.dma_start(T.fc[:, 0:2048], T.fnq[:, 0:512].bitcast(u8)).then_inc(S.stsy, 16)
     store_bc(0)
-    sy.wait_ge(S.sn2, 1)
+    sy.wait_ge(S.fnsc, 1)
     for k in range(4):
         sy.dma_start(T.fs[4 * k:4 * k + 4, 0:512], T.fns[32 * k:32 * k + 4, 0:512]).then_inc(S.stsy, 16)
     store_bc(1)

@@ -5,38 +5,36 @@ N = 4
 CAPP = 128
 TOK = 512
 XA = 336
-RUNS = ((0, 320), (320, 512))
-COPY_V = ((0, 2), (0, 3), (1, 0), (1, 3))
-COPY_S = ((0, 0), (0, 1), (1, 1), (1, 2))
+PART = 32
+ZV = 480
+RUNS = ((0, 256), (256, 512))
+COPY_V = (2, 3)
+COPY_S = (0, 1)
 
 SCRATCH = {
     "xt": ("sbuf", [128, 4 * TOK], "bfloat16"),
     "sn2": ("sbuf", [32, 32], "int32"),
     "lst": ("sbuf", [128, 32], "uint16"),
-    "dm": ("dram", [4, 520], "int32"),
-    "m2": ("sbuf", [32, 128], "int32"),
+    "m2": ("sbuf", [32, 4, 32], "int32"),
     "lp": ("sbuf", [128, 32], "uint16"),
-    "zi": ("sbuf", [128, 32], "int32"),
-    "ca": ("sbuf", [128, 32], "int32"),
-    "cb": ("sbuf", [128, 32], "int32"),
-    "cc": ("sbuf", [128, 32], "int32"),
-    "cl": ("sbuf", [128, 32], "uint16"),
+    "s2": ("sbuf", [64, 32], "int32"),
+    "ln": ("sbuf", [128, 32], "uint16"),
     "ones": ("sbuf", [128, 128], "bfloat16"),
     "ident": ("sbuf", [128, 128], "bfloat16"),
     "et": ("sbuf", [128, 2048], "bfloat16"),
-    "pp": ("psum", [128, 4096], "float32"),
+    "pp": ("psum", [128, 2048], "float32"),
     "bt": ("sbuf", [128, 2048], "bfloat16"),
 }
 for _n, _w in (("x", 512), ("slot", 512), ("land", 512), ("e", 512), ("fp", 512), ("fn", 512), ("bt", 512)):
     SCRATCH[_n + "q"] = ("sbuf", [128, _w], "float8_e4m3fn_x4")
     SCRATCH[_n + "s"] = ("sbuf", [128, _w], "uint8")
 SEMAPHORES = (
-    ["x0", "x1", "snl", "dml", "m2l", "stsy", "stsc",
-     "vones", "vez", "sez", "gid", "gz", "sec", "veq", "qx", "vlst", "ownc", "owns",
-     "vca", "vcc", "vcl", "vlp", "snd", "arrc", "arrs", "fnc", "fnsc", "q0", "q1", "cv0", "cv1", "cs0", "cs1"]
+    ["x0", "x1", "snl", "m2l", "s2l", "stsy", "stsc", "vones", "vez", "vea", "vezb", "sez", "gida", "gidb", "veb",
+     "veqa", "veqb", "arre", "qx", "vlst", "ownc", "owns",
+     "vln", "vlp", "snd", "arrc", "arrs", "fnc", "fnsc", "q0", "q1", "cv", "cs"]
     + ["pc%d" % i for i in range(3)] + ["ps%d" % i for i in range(3)]
-    + ["fc%d" % t for t in range(4)] + ["fs%d" % t for t in range(4)]
-    + ["mm%d%d" % (h, t) for h in range(2) for t in range(4)])
+    + ["fc%d" % h for h in range(2)] + ["fs%d" % h for h in range(2)]
+    + ["mm%d" % t for t in range(4)])
 
 
 def receivers(src, cores, topo):
@@ -74,33 +72,51 @@ def rank_program(g, core, T, topo):
         q.dma_start(T.sn2[16 * k:16 * k + 16, :], T.sn[:]).then_inc(S.snl, 16)
     sy.dma_start(T.xt[:, 0:4 * XA], T.x[:, 0:4 * XA]).then_inc(S.x0, 16)
     sy.dma_start(T.xt[:, 4 * XA:4 * TOK], T.x[:, 4 * XA:4 * TOK]).then_inc(S.x1, 16)
-    for q in range(4):
-        sc.dma_start(T.dm[q:q + 1, 4 - q:516 - q], T.so[:]).then_inc(S.dml, 16)
-    for q in range(1, 4):
-        sc.dma_start(T.dm[q:q + 1, 516 - q:518], T.so[0:1, 0:2 + q]).then_inc(S.dml, 16)
-    sy.wait_ge(S.dml, 112)
     for k in range(2):
-        sy.dma_start(T.m2[16 * k:16 * k + 16, :], T.dm[0:4, 4:516]).then_inc(S.m2l, 16)
+        for q in range(4):
+            r = 16 * k + 4 * q
+            sy.dma_start(T.m2[r:r + 4, :, 0:32 - q], T.so[:, q:32]).then_inc(S.m2l, 16)
+    for k in range(4):
+        sy.dma_start(T.s2[16 * k:16 * k + 16, :], T.so[:]).then_inc(S.s2l, 16)
 
+    plan = receivers(core, T.cores, topo)
+    pal = [dst for dst, _, _ in plan if topo.die(dst) == topo.die(core)][0]
+    low = rank < T.rank_of(pal)
+    first = (0, 128) if low else (TOK - 128, TOK)
+    give = (0, PART) if low else (TOK - PART, TOK)
+    rest = (128, TOK - PART) if low else (PART, TOK - 128)
+    z0, z1 = 4 * rest[0], 4 * rest[1]
     v.memset(T.ones[:], 1.0).then_inc(S.vones, 1)
-    v.memset(T.et[:, 0:1024], 0.0).then_inc(S.vez, 1)
+    v.memset(T.et[:, 4 * first[0]:4 * first[1]], 0.0).then_inc(S.vez, 1)
+    v.memset(T.et[:, z0:z0 + ZV], 0.0).then_inc(S.vezb, 1)
+    sc.wait_ge(S.vezb, 1)
+    parts = range(z0 + ZV, z1, ZV)
+    for a in parts:
+        w = min(ZV, z1 - a)
+        sc.activation(T.et[:, a:a + w], T.et[:, z0:z0 + w], Copy).then_inc(S.sez, 1)
     g.wait_ge(S.vones, 1)
-    g.iota(T.zi[:], [[4, 32]], 0, 128).then_inc(S.gz, 1)
-    g.affine_select(T.ident[:], T.ones[:], [[-1, 128]], AluOpType.is_equal, 0.0, 0, 1).then_inc(S.gid, 1)
-    sc.wait_ge(S.vez, 1)
-    sc.activation(T.et[:, 1024:2048], T.et[:, 0:1024], Copy).then_inc(S.sez, 1)
-    sc.wait_ge(S.gid, 1)
-    sc.wait_ge(S.sez, 1)
-    for t in range(4):
-        sc.activation(T.et[:, 5 * t:2048:16], T.ident[:], Copy).then_inc(S.sec, 1)
+    for (lo, hi), sem in ((first, S.gida), (rest, S.gidb)):
+        a, b = lo // 4, hi // 4
+        g.affine_select(T.ident[:, a:b], T.ones[:, a:b], [[-1, b - a]], AluOpType.is_equal, 0.0, -a, 1).then_inc(sem, 1)
 
-    v.wait_ge(S.gz, 1)
-    v.tensor_scalar(T.ca[:], T.zi[:], 508, None, AluOpType.bitwise_and).then_inc(S.vca, 1)
-    v.tensor_scalar(T.cb[:], T.zi[:], 9, 3, AluOpType.logical_shift_right, AluOpType.bitwise_and).then_inc(S.vca, 1)
-    v.wait_ge(S.vca, 2)
-    v.tensor_tensor(T.cc[:], T.ca[:], T.cb[:], AluOpType.add).then_inc(S.vcc, 1)
-    v.wait_ge(S.vcc, 1)
-    v.tensor_copy(T.cl[:], T.cc[:]).then_inc(S.vcl, 1)
+    def ones_of(cols, sem):
+        for t in range(4):
+            v.tensor_copy(T.et[:, 4 * cols[0] + 5 * t:4 * cols[1]:16], T.ident[:, cols[0] // 4:cols[1] // 4]).then_inc(sem, 1)
+
+    v.wait_ge(S.vez, 1)
+    v.wait_ge(S.gida, 1)
+    ones_of(first, S.vea)
+    v.wait_ge(S.vea, 4)
+    v.quantize_mx(T.eq[:, first[0]:first[1]], T.es[:, first[0]:first[1]],
+                  T.et[:, 4 * first[0]:4 * first[1]]).then_inc(S.veqa, 1)
+    rid, pid, _ = topo.addr(pal)
+    every = topo.engines(core, pal)
+    cut = slice(*give)
+    g.wait_ge(S.veqa, 1)
+    for part in (T.eq[:, cut].bitcast(u8), T.es[:, cut]):
+        g.remote_dma_fused([RemoteDMATransfer(dst_ids=[DstId(rid=rid, pnc=pid)], dma_engine_mask=bits(every),
+                                              remote_sem=S.arre, src=part, dst=part)], local_sem=S.snd)
+
     v.wait_ge(S.snl, 32)
     for k in range(4):
         v.tensor_copy(T.lst[32 * k:32 * k + 32, :], T.sn2[:]).then_inc(S.vlst, 1)
@@ -120,7 +136,6 @@ def rank_program(g, core, T, topo):
         sc.activation(scale[:, lo:hi], T.xs[:, 0:TOK].indirect(off), Copy).then_inc(s_sem, 1)
 
     own = slice(CAPP * rank, CAPP * (rank + 1))
-    plan = receivers(core, T.cores, topo)
     codes, scales = [], []
     for i, (dst, ec, es) in enumerate(plan):
         d = T.rank_of(dst)
@@ -140,90 +155,72 @@ def rank_program(g, core, T, topo):
     for i in range(3):
         g.wait_ge(S["ps%d" % i], 1)
     g.remote_dma_fused(scales, local_sem=S.snd)
-    g.wait_ge(S.snd, sum(len(ec) + len(es) for _, ec, es in plan))
+    g.wait_ge(S.snd, 2 * len(every) + sum(len(ec) + len(es) for _, ec, es in plan))
     arrive = [e for src in T.cores for e in receivers(src, T.cores, topo) if e[0] == core]
 
-    v.wait_ge(S.m2l, 32)
+    v.wait_ge(S.gidb, 1)
+    v.wait_ge(S.vezb, 1)
+    v.wait_ge(S.sez, len(parts))
+    ones_of(rest, S.veb)
+    v.wait_ge(S.m2l, 16 * 8)
     for k in range(4):
-        v.tensor_copy(T.lp[32 * k:32 * k + 32, :], T.m2[:, 0:128:4]).then_inc(S.vlp, 1)
-    v.wait_ge(S.sec, 4)
-    v.quantize_mx(T.eq[:, 0:512], T.es[:, 0:512], T.et[:, 0:2048]).then_inc(S.veq, 1)
+        v.tensor_copy(T.lp[32 * k:32 * k + 32, :], T.m2[:, :, 0:32:4]).then_inc(S.vlp, 1)
+    v.wait_ge(S.veb, 4)
+    v.quantize_mx(T.eq[:, rest[0]:rest[1]], T.es[:, rest[0]:rest[1]], T.et[:, z0:z1]).then_inc(S.veqb, 1)
+    v.wait_ge(S.s2l, 16 * 4)
+    for k in range(2):
+        v.tensor_copy(T.ln[64 * k:64 * k + 64, :], T.s2[:]).then_inc(S.vln, 1)
 
-    te.wait_ge(S.veq, 1)
-    for h, (lo, hi) in enumerate(RUNS):
-        for t in range(4):
-            if h == 0:
-                te.wait_ge(S["fc%d" % t], 1)
-                te.wait_ge(S["fs%d" % t], 1)
-            b = 512 * (4 * h + t)
-            te.matmul_mx(T.pp[:, b:b + hi - lo], T.fpq[:, 128 * t:128 * t + 128], T.fps[:, 128 * t:128 * t + 128],
-                         T.eq[:, lo:hi], T.es[:, lo:hi], True, True).then_inc(S["mm%d%d" % (h, t)], 1)
-
-    def copy_v(h, t):
-        lo, hi = RUNS[h]
-        b = 512 * (4 * h + t)
-        v.wait_ge(S["mm%d%d" % (h, t)], 1)
-        v.tensor_copy(T.bt[:, 4 * lo + t:4 * hi:4], T.pp[:, b:b + hi - lo]).then_inc(S["cv%d" % h], 1)
-
-    def copy_s(h, t):
-        lo, hi = RUNS[h]
-        b = 512 * (4 * h + t)
-        sc.wait_ge(S["mm%d%d" % (h, t)], 1)
-        sc.activation(T.bt[:, 4 * lo + t:4 * hi:4], T.pp[:, b:b + hi - lo], Copy).then_inc(S["cs%d" % h], 1)
+    te.wait_ge(S.veqa, 1)
+    te.wait_ge(S.veqb, 1)
+    te.wait_ge(S.arre, 2 * len(topo.engines(pal, core)))
+    for t in range(4):
+        te.wait_ge(S["fc%d" % (t // 2)], 1)
+        te.wait_ge(S["fs%d" % (t // 2)], 1)
+        te.matmul_mx(T.pp[:, 512 * t:512 * t + 512], T.fpq[:, 128 * t:128 * t + 128], T.fps[:, 128 * t:128 * t + 128],
+                     T.eq[:, 0:512], T.es[:, 0:512], True, True).then_inc(S["mm%d" % t], 1)
 
     v.wait_ge(S.vlp, 4)
     v.wait_ge(S.ownc, 1)
     v.wait_ge(S.arrc, sum(len(ec) for _, ec, _ in arrive))
-    for t in range(4):
-        v.tensor_copy(T.fpq[:, 128 * t:128 * t + 128].bitcast(u32),
-                      T.landq[:, 0:512].bitcast(u32).indirect(T.lp[:, 8 * t:8 * t + 8])).then_inc(S["fc%d" % t], 1)
-    v.wait_ge(S.vcl, 1)
-    for t in range(4):
-        v.wait_ge(S["fc%d" % t], 1)
+    for h in range(2):
+        v.tensor_copy(T.fpq[:, 256 * h:256 * h + 256].bitcast(u32),
+                      T.landq[:, 0:512].bitcast(u32).indirect(T.lp[:, 16 * h:16 * h + 16])).then_inc(S["fc%d" % h], 1)
+    v.wait_ge(S.vln, 2)
     v.tensor_copy(T.fnq[:, 0:512].bitcast(u32),
-                  T.fpq[:, 0:512].bitcast(u32).indirect(T.cl[:, 0:32])).then_inc(S.fnc, 1)
+                  T.landq[:, 0:512].bitcast(u32).indirect(T.ln[:, 0:32])).then_inc(S.fnc, 1)
+    for t in COPY_V:
+        v.wait_ge(S["mm%d" % t], 1)
+        v.tensor_copy(T.bt[:, t:2048:4], T.pp[:, 512 * t:512 * t + 512]).then_inc(S.cv, 1)
+    v.wait_ge(S.cs, len(COPY_S))
+    v.wait_ge(S.cv, len(COPY_V))
     for h, (lo, hi) in enumerate(RUNS):
-        for hh, t in COPY_V:
-            if hh == h:
-                copy_v(h, t)
-        v.wait_ge(S["cv%d" % h], sum(1 for c in COPY_V if c[0] == h))
-        v.wait_ge(S["cs%d" % h], sum(1 for c in COPY_S if c[0] == h))
         v.quantize_mx(T.btq[:, lo:hi], T.bts[:, lo:hi], T.bt[:, 4 * lo:4 * hi]).then_inc(S["q%d" % h], 1)
 
     sc.wait_ge(S.vlp, 4)
     sc.wait_ge(S.owns, 1)
     sc.wait_ge(S.arrs, sum(len(es) for _, _, es in arrive))
-    for t in range(4):
-        sc.activation(T.fps[:, 128 * t:128 * t + 128],
-                      T.lands[:, 0:512].indirect(T.lp[:, 8 * t:8 * t + 8]), Copy).then_inc(S["fs%d" % t], 1)
-    for h, t in COPY_S:
-        if h == 0:
-            copy_s(h, t)
-    sc.wait_ge(S.vcl, 1)
-    for t in range(4):
-        sc.wait_ge(S["fs%d" % t], 1)
-    sc.activation(T.fns[:, 0:512], T.fps[:, 0:512].indirect(T.cl[:, 0:32]), Copy).then_inc(S.fnsc, 1)
-    for h, t in COPY_S:
-        if h == 1:
-            copy_s(h, t)
-
-    def store_bc(h):
-        lo, hi = RUNS[h]
-        sy.wait_ge(S["q%d" % h], 1)
-        sy.dma_start(T.bc[:, 4 * lo:4 * hi], T.btq[:, lo:hi].bitcast(u8)).then_inc(S.stsy, 16)
+    for h in range(2):
+        sc.activation(T.fps[:, 256 * h:256 * h + 256],
+                      T.lands[:, 0:512].indirect(T.lp[:, 16 * h:16 * h + 16]), Copy).then_inc(S["fs%d" % h], 1)
+    for t in COPY_S:
+        sc.wait_ge(S["mm%d" % t], 1)
+        sc.activation(T.bt[:, t:2048:4], T.pp[:, 512 * t:512 * t + 512], Copy).then_inc(S.cs, 1)
+    sc.wait_ge(S.vln, 2)
+    sc.activation(T.fns[:, 0:512], T.lands[:, 0:512].indirect(T.ln[:, 0:32]), Copy).then_inc(S.fnsc, 1)
 
     sy.wait_ge(S.fnc, 1)
     sy.dma_start(T.fc[:, 0:2048], T.fnq[:, 0:512].bitcast(u8)).then_inc(S.stsy, 16)
-    store_bc(0)
-    sy.wait_ge(S.fnsc, 1)
+    for h, (lo, hi) in enumerate(RUNS):
+        sy.wait_ge(S["q%d" % h], 1)
+        sy.dma_start(T.bc[:, 4 * lo:4 * hi], T.btq[:, lo:hi].bitcast(u8)).then_inc(S.stsy, 16)
+    for k in range(3):
+        sy.dma_start(T.bs[4 * k:4 * k + 4, 0:512], T.bts[32 * k:32 * k + 4, 0:512]).then_inc(S.stsy, 16)
+    sc.wait_ge(S.fnsc, 1)
     for k in range(4):
-        sy.dma_start(T.fs[4 * k:4 * k + 4, 0:512], T.fns[32 * k:32 * k + 4, 0:512]).then_inc(S.stsy, 16)
-    store_bc(1)
-    sy.wait_ge(S.q0, 1)
-    sy.dma_start(T.bs[12:16, 0:512], T.bts[96:100, 0:512]).then_inc(S.stsy, 16)
+        sc.dma_start(T.fs[4 * k:4 * k + 4, 0:512], T.fns[32 * k:32 * k + 4, 0:512]).then_inc(S.stsc, 16)
     sc.wait_ge(S.q0, 1)
     sc.wait_ge(S.q1, 1)
-    for k in range(3):
-        sc.dma_start(T.bs[4 * k:4 * k + 4, 0:512], T.bts[32 * k:32 * k + 4, 0:512]).then_inc(S.stsc, 16)
-    sy.wait_ge(S.stsy, 16 * 8)
-    sc.wait_ge(S.stsc, 16 * 3)
+    sc.dma_start(T.bs[12:16, 0:512], T.bts[96:100, 0:512]).then_inc(S.stsc, 16)
+    sy.wait_ge(S.stsy, 16 * 6)
+    sc.wait_ge(S.stsc, 16 * 5)

from concourse.bass import DstId, RemoteDMATransfer
from concourse.mybir import dt, AluOpType, ActivationFunctionType

N = 4
CAPP = 128
TOK = 512
XA = 336
PART = 32
ZV = 480
RUNS = ((0, 256), (256, 512))
COPY_V = (2, 3)
COPY_S = (0, 1)

SCRATCH = {
    "xt": ("sbuf", [128, 4 * TOK], "bfloat16"),
    "sn2": ("sbuf", [32, 32], "int32"),
    "lst": ("sbuf", [128, 32], "uint16"),
    "m2": ("sbuf", [32, 4, 32], "int32"),
    "lp": ("sbuf", [128, 32], "uint16"),
    "s2": ("sbuf", [64, 32], "int32"),
    "ln": ("sbuf", [128, 32], "uint16"),
    "ones": ("sbuf", [128, 128], "bfloat16"),
    "ident": ("sbuf", [128, 128], "bfloat16"),
    "et": ("sbuf", [128, 2048], "bfloat16"),
    "pp": ("psum", [128, 2048], "float32"),
    "bt": ("sbuf", [128, 2048], "bfloat16"),
}
for _n, _w in (("x", 512), ("slot", 512), ("land", 512), ("e", 512), ("fp", 512), ("fn", 512), ("bt", 512)):
    SCRATCH[_n + "q"] = ("sbuf", [128, _w], "float8_e4m3fn_x4")
    SCRATCH[_n + "s"] = ("sbuf", [128, _w], "uint8")
SEMAPHORES = (
    ["x0", "x1", "snl", "m2l", "s2l", "stsy", "stsc", "vones", "vez", "vea", "vezb", "sez", "gida", "gidb", "veb",
     "veqa", "veqb", "arre", "qx", "vlst", "ownc", "owns",
     "vln", "vlp", "snd", "arrc", "arrs", "fnc", "fnsc", "q0", "q1", "cv", "cs"]
    + ["pc%d" % i for i in range(3)] + ["ps%d" % i for i in range(3)]
    + ["fc%d" % h for h in range(2)] + ["fs%d" % h for h in range(2)]
    + ["mm%d" % t for t in range(4)])


def receivers(src, cores, topo):
    mine = [c for c in cores if topo.die(c) == topo.die(src)]
    far = [c for c in cores if topo.die(c) != topo.die(src)]
    k = mine.index(src)
    far = far[k:] + far[:k]
    near = [c for c in mine if c != src]
    out = []
    for i, c in enumerate(far[:1] + near + far[1:]):
        e = topo.engines(src, c)
        a, b = e[0::2], e[1::2]
        h = len(b) // 2
        out.append((c, (a, b, a)[i], (b[:h], a, b[h:])[i]))
    return out


def bits(engines):
    m = 0
    for e in engines:
        m |= 1 << e
    return m


def rank_program(g, core, T, topo):
    rank = T.rank_of(core)
    if rank is None:
        return
    S = T.sem
    v, sc, te, sy = g.vector, g.scalar, g.tensor, g.sync
    Copy = ActivationFunctionType.Copy
    u32, u8 = dt.uint32, dt.uint8

    for k, q in enumerate((sy, sc)):
        q.dma_start(T.sn2[16 * k:16 * k + 16, :], T.sn[:]).then_inc(S.snl, 16)
    sy.dma_start(T.xt[:, 0:4 * XA], T.x[:, 0:4 * XA]).then_inc(S.x0, 16)
    sy.dma_start(T.xt[:, 4 * XA:4 * TOK], T.x[:, 4 * XA:4 * TOK]).then_inc(S.x1, 16)
    for k in range(2):
        for q in range(4):
            r = 16 * k + 4 * q
            sy.dma_start(T.m2[r:r + 4, :, 0:32 - q], T.so[:, q:32]).then_inc(S.m2l, 16)
    for k in range(4):
        sy.dma_start(T.s2[16 * k:16 * k + 16, :], T.so[:]).then_inc(S.s2l, 16)

    plan = receivers(core, T.cores, topo)
    pal = [dst for dst, _, _ in plan if topo.die(dst) == topo.die(core)][0]
    low = rank < T.rank_of(pal)
    first = (0, 128) if low else (TOK - 128, TOK)
    give = (0, PART) if low else (TOK - PART, TOK)
    rest = (128, TOK - PART) if low else (PART, TOK - 128)
    z0, z1 = 4 * rest[0], 4 * rest[1]
    v.memset(T.ones[:], 1.0).then_inc(S.vones, 1)
    v.memset(T.et[:, 4 * first[0]:4 * first[1]], 0.0).then_inc(S.vez, 1)
    v.memset(T.et[:, z0:z0 + ZV], 0.0).then_inc(S.vezb, 1)
    sc.wait_ge(S.vezb, 1)
    parts = range(z0 + ZV, z1, ZV)
    for a in parts:
        w = min(ZV, z1 - a)
        sc.activation(T.et[:, a:a + w], T.et[:, z0:z0 + w], Copy).then_inc(S.sez, 1)
    g.wait_ge(S.vones, 1)
    for (lo, hi), sem in ((first, S.gida), (rest, S.gidb)):
        a, b = lo // 4, hi // 4
        g.affine_select(T.ident[:, a:b], T.ones[:, a:b], [[-1, b - a]], AluOpType.is_equal, 0.0, -a, 1).then_inc(sem, 1)

    def ones_of(cols, sem):
        for t in range(4):
            v.tensor_copy(T.et[:, 4 * cols[0] + 5 * t:4 * cols[1]:16], T.ident[:, cols[0] // 4:cols[1] // 4]).then_inc(sem, 1)

    v.wait_ge(S.vez, 1)
    v.wait_ge(S.gida, 1)
    ones_of(first, S.vea)
    v.wait_ge(S.vea, 4)
    v.quantize_mx(T.eq[:, first[0]:first[1]], T.es[:, first[0]:first[1]],
                  T.et[:, 4 * first[0]:4 * first[1]]).then_inc(S.veqa, 1)
    rid, pid, _ = topo.addr(pal)
    every = topo.engines(core, pal)
    cut = slice(*give)
    g.wait_ge(S.veqa, 1)
    for part in (T.eq[:, cut].bitcast(u8), T.es[:, cut]):
        g.remote_dma_fused([RemoteDMATransfer(dst_ids=[DstId(rid=rid, pnc=pid)], dma_engine_mask=bits(every),
                                              remote_sem=S.arre, src=part, dst=part)], local_sem=S.snd)

    v.wait_ge(S.snl, 32)
    for k in range(4):
        v.tensor_copy(T.lst[32 * k:32 * k + 32, :], T.sn2[:]).then_inc(S.vlst, 1)
    v.wait_ge(S.x0, 16)
    v.quantize_mx(T.xq[:, 0:XA], T.xs[:, 0:XA], T.xt[:, 0:4 * XA]).then_inc(S.qx, 1)
    v.wait_ge(S.x1, 16)
    v.quantize_mx(T.xq[:, XA:TOK], T.xs[:, XA:TOK], T.xt[:, 4 * XA:4 * TOK]).then_inc(S.qx, 1)

    for q in (v, sc):
        q.wait_ge(S.vlst, 4)
        q.wait_ge(S.qx, 2)

    def pick(d, code, scale, c_sem, s_sem):
        lo, hi = CAPP * d, CAPP * (d + 1)
        off = T.lst[:, 8 * d:8 * d + 8]
        v.tensor_copy(code[:, lo:hi].bitcast(u32), T.xq[:, 0:TOK].bitcast(u32).indirect(off)).then_inc(c_sem, 1)
        sc.activation(scale[:, lo:hi], T.xs[:, 0:TOK].indirect(off), Copy).then_inc(s_sem, 1)

    own = slice(CAPP * rank, CAPP * (rank + 1))
    codes, scales = [], []
    for i, (dst, ec, es) in enumerate(plan):
        d = T.rank_of(dst)
        pick(d, T.slotq, T.slots, S["pc%d" % i], S["ps%d" % i])
        rid, pid, _ = topo.addr(dst)
        cut = slice(CAPP * d, CAPP * (d + 1))
        codes.append(RemoteDMATransfer(dst_ids=[DstId(rid=rid, pnc=pid)], dma_engine_mask=bits(ec), remote_sem=S.arrc,
                                       src=T.slotq[:, cut].bitcast(u8), dst=T.landq[:, own].bitcast(u8)))
        scales.append(RemoteDMATransfer(dst_ids=[DstId(rid=rid, pnc=pid)], dma_engine_mask=bits(es), remote_sem=S.arrs,
                                        src=T.slots[:, cut], dst=T.lands[:, own]))
    pick(rank, T.landq, T.lands, S.ownc, S.owns)
    g.wait_ge(S.pc0, 1)
    g.remote_dma_fused(codes[:1], local_sem=S.snd)
    g.wait_ge(S.pc1, 1)
    g.wait_ge(S.pc2, 1)
    g.remote_dma_fused(codes[1:], local_sem=S.snd)
    for i in range(3):
        g.wait_ge(S["ps%d" % i], 1)
    g.remote_dma_fused(scales, local_sem=S.snd)
    g.wait_ge(S.snd, 2 * len(every) + sum(len(ec) + len(es) for _, ec, es in plan))
    arrive = [e for src in T.cores for e in receivers(src, T.cores, topo) if e[0] == core]

    v.wait_ge(S.gidb, 1)
    v.wait_ge(S.vezb, 1)
    v.wait_ge(S.sez, len(parts))
    ones_of(rest, S.veb)
    v.wait_ge(S.m2l, 16 * 8)
    for k in range(4):
        v.tensor_copy(T.lp[32 * k:32 * k + 32, :], T.m2[:, :, 0:32:4]).then_inc(S.vlp, 1)
    v.wait_ge(S.veb, 4)
    v.quantize_mx(T.eq[:, rest[0]:rest[1]], T.es[:, rest[0]:rest[1]], T.et[:, z0:z1]).then_inc(S.veqb, 1)
    v.wait_ge(S.s2l, 16 * 4)
    for k in range(2):
        v.tensor_copy(T.ln[64 * k:64 * k + 64, :], T.s2[:]).then_inc(S.vln, 1)

    te.wait_ge(S.veqa, 1)
    te.wait_ge(S.veqb, 1)
    te.wait_ge(S.arre, 2 * len(topo.engines(pal, core)))
    for t in range(4):
        te.wait_ge(S["fc%d" % (t // 2)], 1)
        te.wait_ge(S["fs%d" % (t // 2)], 1)
        te.matmul_mx(T.pp[:, 512 * t:512 * t + 512], T.fpq[:, 128 * t:128 * t + 128], T.fps[:, 128 * t:128 * t + 128],
                     T.eq[:, 0:512], T.es[:, 0:512], True, True).then_inc(S["mm%d" % t], 1)

    v.wait_ge(S.vlp, 4)
    v.wait_ge(S.ownc, 1)
    v.wait_ge(S.arrc, sum(len(ec) for _, ec, _ in arrive))
    for h in range(2):
        v.tensor_copy(T.fpq[:, 256 * h:256 * h + 256].bitcast(u32),
                      T.landq[:, 0:512].bitcast(u32).indirect(T.lp[:, 16 * h:16 * h + 16])).then_inc(S["fc%d" % h], 1)
    v.wait_ge(S.vln, 2)
    v.tensor_copy(T.fnq[:, 0:512].bitcast(u32),
                  T.landq[:, 0:512].bitcast(u32).indirect(T.ln[:, 0:32])).then_inc(S.fnc, 1)
    for t in COPY_V:
        v.wait_ge(S["mm%d" % t], 1)
        v.tensor_copy(T.bt[:, t:2048:4], T.pp[:, 512 * t:512 * t + 512]).then_inc(S.cv, 1)
    v.wait_ge(S.cs, len(COPY_S))
    v.wait_ge(S.cv, len(COPY_V))
    for h, (lo, hi) in enumerate(RUNS):
        v.quantize_mx(T.btq[:, lo:hi], T.bts[:, lo:hi], T.bt[:, 4 * lo:4 * hi]).then_inc(S["q%d" % h], 1)

    sc.wait_ge(S.vlp, 4)
    sc.wait_ge(S.owns, 1)
    sc.wait_ge(S.arrs, sum(len(es) for _, _, es in arrive))
    for h in range(2):
        sc.activation(T.fps[:, 256 * h:256 * h + 256],
                      T.lands[:, 0:512].indirect(T.lp[:, 16 * h:16 * h + 16]), Copy).then_inc(S["fs%d" % h], 1)
    for t in COPY_S:
        sc.wait_ge(S["mm%d" % t], 1)
        sc.activation(T.bt[:, t:2048:4], T.pp[:, 512 * t:512 * t + 512], Copy).then_inc(S.cs, 1)
    sc.wait_ge(S.vln, 2)
    sc.activation(T.fns[:, 0:512], T.lands[:, 0:512].indirect(T.ln[:, 0:32]), Copy).then_inc(S.fnsc, 1)

    sy.wait_ge(S.fnc, 1)
    sy.dma_start(T.fc[:, 0:2048], T.fnq[:, 0:512].bitcast(u8)).then_inc(S.stsy, 16)
    for h, (lo, hi) in enumerate(RUNS):
        sy.wait_ge(S["q%d" % h], 1)
        sy.dma_start(T.bc[:, 4 * lo:4 * hi], T.btq[:, lo:hi].bitcast(u8)).then_inc(S.stsy, 16)
    for k in range(3):
        sy.dma_start(T.bs[4 * k:4 * k + 4, 0:512], T.bts[32 * k:32 * k + 4, 0:512]).then_inc(S.stsy, 16)
    sc.wait_ge(S.fnsc, 1)
    for k in range(4):
        sc.dma_start(T.fs[4 * k:4 * k + 4, 0:512], T.fns[32 * k:32 * k + 4, 0:512]).then_inc(S.stsc, 16)
    sc.wait_ge(S.q0, 1)
    sc.wait_ge(S.q1, 1)
    sc.dma_start(T.bs[12:16, 0:512], T.bts[96:100, 0:512]).then_inc(S.stsc, 16)
    sy.wait_ge(S.stsy, 16 * 6)
    sc.wait_ge(S.stsc, 16 * 5)
